import numpy as np
import ml_dtypes


def mxq(x, axis, fmt="e4m3"):
    dtype, down = {"e4m3": (ml_dtypes.float8_e4m3fn, 7), "e5m2": (ml_dtypes.float8_e5m2, 14)}[fmt]
    v = np.moveaxis(np.asarray(x, np.float32).astype(ml_dtypes.bfloat16).astype(np.float64), axis, -1)
    blocks = v.reshape(v.shape[:-1] + (-1, 32))
    amax = np.abs(blocks).max(-1, keepdims=True)
    byte = np.maximum(np.where(amax > 0, np.frexp(amax)[1] - 1 + 127, 0) - down, 1)
    scale = np.exp2(byte - 127.0)
    codes = (blocks / scale).astype(np.float32).astype(dtype).astype(np.float64)
    return np.moveaxis((codes * scale).reshape(v.shape), -1, axis)


WIDE = False


def mx_kscale(k):
    if not WIDE:
        return np.ones(k)
    levels = np.array([10, -10, 5, -5, 0])
    if k % 512:
        return np.exp2(np.random.permutation(np.resize(levels, k // 32))).repeat(32)
    a = np.empty((k // 512, 16))
    for p in range(k // 512):
        a[p, :8] = np.random.permutation(np.resize(levels, 8))
        for g in range(8):
            far = levels[np.abs(levels - a[p, g]) >= 10]
            a[p, g + 8] = far[np.random.randint(len(far))]
    return np.exp2(a.ravel()).repeat(32)


def f64(x):
    return np.asarray(x).astype(np.float64)


def striped(idx):
    return np.tile(idx.reshape(-1, 16).T, (8, 1)).astype(np.uint16)


def unstriped(offs):
    return offs[:16].T.reshape(-1).astype(np.int64)


E2M1 = np.array([0.0, 0.5, 1.0, 1.5, 2.0, 3.0, 4.0, 6.0, -0.0, -0.5, -1.0, -1.5, -2.0, -3.0, -4.0, -6.0])


def pack_weight(w, fmt):
    k, n = w.shape
    w = f64(np.asarray(w, np.float32).astype(ml_dtypes.bfloat16)).reshape(k // 32, 32, n)
    amax = np.abs(w).max(1)
    if fmt == "e4m3":
        byte = np.frexp(amax)[1] - 1 + 127 - 7
    else:
        mant, ex = np.frexp(amax / 6.0)
        byte = np.where(mant > 0.5, ex, ex - 1) + 127
    byte = np.clip(np.where(amax > 0, byte, 1), 1, 254)
    scaled = (w * np.exp2(127.0 - byte)[:, None, :]).reshape(k, n).astype(np.float32)
    by_word = np.ascontiguousarray(scaled.reshape(k // 512, 128, 4, n).transpose(0, 1, 3, 2))
    if fmt == "e4m3":
        words = by_word.astype(ml_dtypes.float8_e4m3fn).view(np.uint8)
    else:
        c = by_word.astype(ml_dtypes.float4_e2m1fn).view(np.uint8) & 0xF
        words = (c[..., 0::2] | (c[..., 1::2] << 4)).reshape(k // 512, 128, 2 * n)
    return np.ascontiguousarray(words), np.ascontiguousarray(byte.astype(np.uint8).reshape(k // 512, 16, n))


def unpack_weight(words, scales, fmt):
    g, _, n = scales.shape
    words = np.ascontiguousarray(words).reshape(g, 128, n, -1)
    if fmt == "e4m3":
        vals = words.view(ml_dtypes.float8_e4m3fn).astype(np.float64)
    else:
        nib = np.empty((g, 128, n, 4), np.uint8)
        nib[..., 0::2] = words & 0xF
        nib[..., 1::2] = words >> 4
        vals = E2M1[nib]
    vals = vals * np.repeat(np.exp2(scales.astype(np.float64) - 127.0), 8, axis=1)[..., None]
    return vals.transpose(0, 1, 3, 2).reshape(g * 512, n)


def silu(v):
    return v / (1.0 + np.exp(-np.maximum(v, -700.0)))


K, T, E, C, H, N = 2560, 640, 2, 256, 1024, 512


def by_expert(wq, xq):
    return np.concatenate([wq[e].T @ xq[:, e * C:(e + 1) * C] for e in range(E)], axis=1)


def setup_inputs():
    n = np.random.standard_normal
    s = mx_kscale(K)[:, None]
    u = mx_kscale(H)
    w1 = [pack_weight(m, "e2m1") for m in n((E, K, H)) / np.sqrt(K) / s[None] * u[None, None, :]]
    w2 = [pack_weight(m, "e2m1") for m in n((E, H, N)) / np.sqrt(H) / u[None, :, None]]
    x = pack_weight(n((K, T)) * s, "e4m3")
    return {
        "x_words": x[0],
        "x_scales": x[1],
        "w1_words": np.stack([m[0] for m in w1]),
        "w1_scales": np.stack([m[1] for m in w1]),
        "w2_words": np.stack([m[0] for m in w2]),
        "w2_scales": np.stack([m[1] for m in w2]),
        "gate": np.tile(np.random.uniform(0.2, 1.0, E * C), (N, 1)).astype(np.float32),
        "offs": striped(np.random.permutation(T)[:E * C]),
    }


def reference(x_words, x_scales, w1_words, w1_scales, w2_words, w2_scales, gate, offs):
    idx = unstriped(offs)
    w1 = np.stack([unpack_weight(w1_words[e], w1_scales[e], "e2m1") for e in range(E)])
    w2 = np.stack([unpack_weight(w2_words[e], w2_scales[e], "e2m1") for e in range(E)])
    xq = unpack_weight(x_words, x_scales, "e4m3")[:, idx]
    h = silu(by_expert(w1, xq))
    y = by_expert(w2, mxq(h, 0, "e4m3"))
    out = np.zeros((N, T))
    out[:, idx] = f64(gate) * y
    return out

@@ -1,0 +1,241 @@
+from contextlib import ExitStack
+
+import concourse.mybir as mybir
+
+K, T, E, C, H, N = 2560, 640, 2, 256, 1024, 512
+FLOPS = 2 * E * C * (K * H + H * N)
+
+F32, BF16 = mybir.dt.float32, mybir.dt.bfloat16
+I32, U32, U16, U8 = mybir.dt.int32, mybir.dt.uint32, mybir.dt.uint16, mybir.dt.uint8
+FP8X4, FP4X4 = mybir.dt.float8_e4m3fn_x4, mybir.dt.float4_e2m1fn_x4
+SILU = mybir.ActivationFunctionType.Silu
+MULT = mybir.AluOpType.mult
+
+P = 128
+PASS = 512
+KP, HP = K // PASS, H // PASS
+NT = N // P
+ST = C // P
+T_PAD = 704
+HOLD = 3
+
+
+def tile_moe_pkd_mlp_silu_kernel(
+    tc, x_words, x_scales, w1_words, w1_scales, w2_words, w2_scales, gate, offs, out
+):
+    nc = tc.nc
+    with ExitStack() as ctx:
+        keep = ctx.enter_context(tc.tile_pool(name="keep", bufs=1))
+        staged = ctx.enter_context(tc.tile_pool(name="staged", bufs=1))
+        psum = ctx.enter_context(tc.psum_pool(name="psum", bufs=1))
+
+        def sb(name, shape, dtype, tag=None):
+            return keep.tile(shape, dtype, name=name, tag=tag or name, align_bytes=64)
+
+        def scale_plane(name, passes, width):
+            plane = sb(name, [P, passes * width], U8)
+            nc.vector.memset(plane[:].bitcast(I32), 0)
+            return plane
+
+        def load_scales(plane, rows, passes):
+            src = rows.bitcast(I32).rearrange("a (q r) w -> r q a w", r=4)
+            dst = plane[:].bitcast(I32).rearrange("p (a w) -> p a w", a=passes)
+            for r in range(4):
+                nc.sync.dma_start(out=dst[r:P:32], in_=src[r])
+
+        offsets = keep.tile([P, E * C // 16], U16, name="offsets")
+        def placed(name, shape, dtype, offset):
+            return staged.tile(shape, dtype, name=name, align_bytes=64, offset=offset)
+
+        XB, WB = 4 * T, 2 * H
+        second = XB + 2 * WB
+        third = 3 * XB + 3 * WB + KP * WB + E * HP * 2 * N + 4 * E * C + E * HP * N + KP * H + 4 * C
+        xs_rest = placed("xs_rest", [P, third], U8, second)
+        nc.gpsimd.memset(xs_rest[:, 0:T_PAD].bitcast(I32), 0)
+        xs0 = sb("xs0", [P, T], U8)
+        nc.gpsimd.memset(xs0[:].bitcast(I32), 0)
+        w1s = [scale_plane("w1s0", KP, H)]
+        blank = placed("blank", [P, second // 4], F32, 0)
+        nc.vector.memset(blank[:, 0:P], 0.0)
+        ident = sb("ident", [P, P], F32)
+        nc.gpsimd.affine_select(
+            out=ident[:], in_=blank[:, 0:P], compare_op=mybir.AluOpType.not_equal, fill=1.0, base=0,
+            pattern=[[-1, P]], channel_multiplier=1,
+        )
+        zero = sb("zero", [P, 1], F32)
+        nc.vector.memset(zero[:], 0.0)
+        moved = scale_plane("moved", KP - 1, E * C)
+
+        cursor = [0]
+
+        def following(name, shape, dtype, size):
+            tile = placed(name, shape, dtype, cursor[0])
+            cursor[0] = cursor[0] + size
+            return tile
+
+        xw, w1, w2 = {}, {}, {}
+
+        def load_x(a, tile):
+            xw[a] = tile
+            nc.sync.dma_start(out=tile[:], in_=x_words[a].rearrange("p t r -> p (t r)").bitcast(I32))
+
+        def load_w1(e, a):
+            w1[e, a] = following("w1_%d_%d" % (e, a), [P, WB], U8, WB)
+            nc.sync.dma_start(out=w1[e, a][:].bitcast(I32), in_=w1_words[e, a].bitcast(I32))
+
+        def load_w2(e):
+            w2[e] = following("w2_%d" % e, [P, HP * 2 * N], U8, HP * 2 * N)
+            nc.sync.dma_start(
+                out=w2[e][:].bitcast(I32).rearrange("p (g w) -> p g w", g=HP),
+                in_=w2_words[e].bitcast(I32).rearrange("g p w -> p g w"),
+            )
+
+        nc.sync.dma_start(offsets[:], offs)
+        load_x(0, sb("xw0", [P, T], I32))
+        nc.sync.dma_start(
+            out=xs_rest[0:64, 0:T].bitcast(I32), in_=x_scales[1:KP].bitcast(I32).rearrange("a f w -> f a w")
+        )
+        load_scales(xs0, x_scales[0:1], 1)
+        load_scales(w1s[0], w1_scales[0], KP)
+        load_w1(0, 0)
+        load_x(1, following("xw1", [P, T], I32, XB))
+        load_w1(0, 1)
+        assert cursor[0] == second
+        rest = sb("rest", [P, E * C], U8)
+        nc.vector.tensor_copy(rest[:], xs_rest[:, 0:T_PAD].indirect(offsets[:]))
+        for q in range(4):
+            nc.sync.dma_start(
+                out=moved[32 * q:32 * q + 4, :].bitcast(I32), in_=rest[16 * q:16 * (q + 1), :].bitcast(I32)
+            )
+        w2s = following("w2s", [P, E * HP * N], U8, E * HP * N)
+        w1s.append(following("w1s1", [P, KP * H], U8, KP * H))
+        for plane in (w2s, w1s[1]):
+            nc.gpsimd.memset(plane[:].bitcast(I32), 0)
+        for a in range(2, KP):
+            load_x(a, following("xw%d" % a, [P, T], I32, XB))
+            load_w1(0, a)
+        load_w2(0)
+        load_scales(w2s, w2_scales.rearrange("e g q w -> (e g) q w"), E * HP)
+        gate_sb = following("gate_sb", [P, E * C], F32, 4 * E * C)
+        nc.sync.dma_start(out=gate_sb[:], in_=gate[0:P, :])
+        for a in range(KP):
+            load_w1(1, a)
+        load_scales(w1s[1], w1_scales[1], KP)
+        load_w2(1)
+        gw_first = following("gw0_0", [P, C], U32, 4 * C)
+        assert cursor[0] == second + third
+
+        def lst(first, count):
+            return offsets[:, first // 16:(first + count) // 16]
+
+        def gather_words(dst, a, first, count):
+            nc.vector.tensor_copy(dst, xw[a][:].bitcast(U32).indirect(lst(first, count)))
+
+        def hidden(acc_t, e, t):
+            name = "%d_%d" % (e, t)
+            hb = sb("hb" + name, [P, H], BF16)
+            turned = psum.tile([P, HP, 2, P], F32, name="turned" + name, tag="turned", bufs=2)
+            for h in range(HP):
+                nc.scalar.activation(
+                    out=hb[:, h * PASS:(h + 1) * PASS].rearrange("s (u m j) -> s u m j", u=2, j=2),
+                    in_=acc_t[h][:].rearrange("s (m u j) -> s u m j", u=2, j=2),
+                    func=SILU,
+                )
+                for u in range(2):
+                    lo = h * 2 * P + u * P
+                    nc.tensor.transpose(turned[:, h, u, :], hb[:].bitcast(F32)[:, lo:lo + P], ident[:])
+            grouped = sb("grouped" + name, [P, HP * P * 4], BF16)
+            nc.scalar.copy(
+                out=grouped[:].bitcast(F32).rearrange("p (g s u) -> p g s u", g=HP, u=2),
+                in_=turned[:].rearrange("p g u s -> p g s u"),
+            )
+            codes = sb("hc" + name, [P, HP * P], U32)
+            scales = sb("hs" + name, [P, HP * P], U8)
+            nc.vector.quantize_mx(out=codes[:].bitcast(FP8X4), scales=scales[:], in_=grouped[:])
+            return codes, scales
+
+        def layer2(e, t, codes, scales):
+            y = psum.tile([P, NT, P], F32, name="y%d_%d" % (e, t), tag="y", bufs=2)
+            for n in range(NT):
+                for g in range(HP):
+                    nc.tensor.matmul_mx(
+                        out=y[:, n, :],
+                        lhsT=w2[e][:, g * 2 * N + n * 2 * P:g * 2 * N + (n + 1) * 2 * P].bitcast(FP4X4),
+                        lhsT_scale=w2s[:, (e * HP + g) * N + n * P:(e * HP + g) * N + (n + 1) * P],
+                        rhs=codes[:, g * P:(g + 1) * P].bitcast(FP8X4),
+                        rhs_scale=scales[:, g * P:(g + 1) * P],
+                        start=(g == 0),
+                        stop=(g == HP - 1),
+                    )
+            return y
+
+        def scatter(j, n, src):
+            nc.vector.tensor_tensor(
+                res[n][:].indirect(offsets[:, j * P // 16:(j + 1) * P // 16]), src, gate_sb[:, j * P:(j + 1) * P], MULT
+            )
+
+        res = [sb("res%d" % n, [P, T], F32) for n in range(NT)]
+        for n in range(NT):
+            nc.scalar.activation(out=res[n][:], in_=zero[:].to_broadcast([P, T]), func=SILU)
+
+
+        gb = [sb("gb%d" % e, [P, C], U8) for e in range(E)]
+        gw = {}
+        for a in range(KP):
+            if a == HOLD:
+                for t in range(ST):
+                    gw[t, a] = sb("gw0_%d_%d" % (a, t), [P, P], U32)[:]
+                    gather_words(gw[t, a], a, t * P, P)
+            else:
+                both = sb("gw0_%d" % a, [P, C], U32) if a else gw_first
+                gather_words(both[:], a, 0, C)
+                for t in range(ST):
+                    gw[t, a] = both[:, t * P:(t + 1) * P]
+            if a == 0:
+                for e in range(E):
+                    nc.vector.tensor_copy(gb[e][:], xs0[:].indirect(lst(e * C, C)))
+
+        def token_scales(j, a):
+            if a == 0:
+                return gb[j // ST][:, (j % ST) * P:(j % ST + 1) * P]
+            return moved[:, (a - 1) * E * C + j * P:(a - 1) * E * C + (j + 1) * P]
+
+        half = NT // 2
+        before = None
+        for j in range(E * ST):
+            e, t = divmod(j, ST)
+            acc = [psum.tile([P, PASS], F32, name="acc%d_%d" % (j, h), tag="acc", bufs=4) for h in range(HP)]
+            for a in range(KP):
+                for h in range(HP):
+                    nc.tensor.matmul_mx(
+                        out=acc[h][:],
+                        lhsT=gw[j, a].bitcast(FP8X4),
+                        lhsT_scale=token_scales(j, a),
+                        rhs=w1[e, a][:, h * 2 * PASS:(h + 1) * 2 * PASS].bitcast(FP4X4),
+                        rhs_scale=w1s[e][:, a * H + h * PASS:a * H + (h + 1) * PASS],
+                        start=(a == 0),
+                        stop=(a == KP - 1),
+                    )
+            if j == 0:
+                held = sb("gw1", [P, KP * C], U32, tag="gw0_%d_0" % HOLD)
+                for a in range(KP):
+                    gather_words(held[:, a * C:(a + 1) * C], a, C, C)
+                    for i in range(ST):
+                        gw[ST + i, a] = held[:, a * C + i * P:a * C + (i + 1) * P]
+            codes, scales = hidden(acc, e, t)
+            if before is not None:
+                late = sb("late%d" % j, [P, half, P], F32, tag="hb%d_%d" % (e, t))
+                nc.scalar.copy(out=late[:], in_=before[:, half:NT, :])
+                for n in range(half, NT):
+                    scatter(j - 1, n, late[:, n - half, :])
+            y = layer2(e, t, codes, scales)
+            last = j == E * ST - 1
+            first_n = NT if last else half
+            early = sb("early%d" % j, [P, first_n, P], F32)
+            nc.scalar.copy(out=early[:], in_=y[:, 0:first_n, :])
+
+            for n in range(first_n):
+                scatter(j, n, early[:, n, :])
+                if last:
+                    nc.sync.dma_start(out=out[n * P:(n + 1) * P, :], in_=res[n][:])
+            before = y

@@ -16,8 +16,8 @@ PASS = 512
 KP, HP = K // PASS, H // PASS
 NT = N // P
 ST = C // P
-T_PAD = 704
-HOLD = 3
+HOLD = 2
+SPLIT = 3
 
 
 def tile_moe_pkd_mlp_silu_kernel(
@@ -48,23 +48,22 @@ def tile_moe_pkd_mlp_silu_kernel(
             return staged.tile(shape, dtype, name=name, align_bytes=64, offset=offset)
 
         XB, WB = 4 * T, 2 * H
-        second = XB + 2 * WB
-        third = 3 * XB + 3 * WB + KP * WB + E * HP * 2 * N + 4 * E * C + E * HP * N + KP * H + 4 * C
-        xs_rest = placed("xs_rest", [P, third], U8, second)
-        nc.gpsimd.memset(xs_rest[:, 0:T_PAD].bitcast(I32), 0)
-        xs0 = sb("xs0", [P, T], U8)
-        nc.gpsimd.memset(xs0[:].bitcast(I32), 0)
-        w1s = [scale_plane("w1s0", KP, H)]
-        blank = placed("blank", [P, second // 4], F32, 0)
-        nc.vector.memset(blank[:, 0:P], 0.0)
+        second = 2 * WB
+        third = 4 * XB + 3 * WB + KP * WB + E * HP * 2 * N + 4 * E * C + KP * H + E * HP * N
+        xs = scale_plane("xs", KP, T)
         ident = sb("ident", [P, P], F32)
-        nc.gpsimd.affine_select(
-            out=ident[:], in_=blank[:, 0:P], compare_op=mybir.AluOpType.not_equal, fill=1.0, base=0,
-            pattern=[[-1, P]], channel_multiplier=1,
-        )
-        zero = sb("zero", [P, 1], F32)
-        nc.vector.memset(zero[:], 0.0)
-        moved = scale_plane("moved", KP - 1, E * C)
+
+        def ident_part(name, offset, end, lo, width, engine):
+            zeros = placed(name, [P, (end - offset) // 4], F32, offset)
+            engine.memset(zeros[:, 0:width], 0.0)
+            nc.gpsimd.affine_select(
+                out=ident[:, lo:lo + width], in_=zeros[:, 0:width], compare_op=mybir.AluOpType.not_equal, fill=1.0,
+                base=-lo, pattern=[[-1, width]], channel_multiplier=1,
+            )
+
+        ident_part("blank0", 0, second, 0, 32, nc.vector)
+        w1s = [scale_plane("w1s0", KP, H)]
+        xs_rest = scale_plane("xs_rest", 1, T)
 
         cursor = [0]
 
@@ -73,68 +72,73 @@ def tile_moe_pkd_mlp_silu_kernel(
             cursor[0] = cursor[0] + size
             return tile
 
-        xw, w1, w2 = {}, {}, {}
+        xw, w1 = {}, {}
 
-        def load_x(a, tile):
-            xw[a] = tile
-            nc.sync.dma_start(out=tile[:], in_=x_words[a].rearrange("p t r -> p (t r)").bitcast(I32))
-
-        def load_w1(e, a):
-            w1[e, a] = following("w1_%d_%d" % (e, a), [P, WB], U8, WB)
-            nc.sync.dma_start(out=w1[e, a][:].bitcast(I32), in_=w1_words[e, a].bitcast(I32))
-
-        def load_w2(e):
-            w2[e] = following("w2_%d" % e, [P, HP * 2 * N], U8, HP * 2 * N)
+        def load_x(lo, hi):
+            if lo == 0:
+                tile = sb("xw0", [P, T], I32)
+            else:
+                tile = following("xw%d" % lo, [P, (hi - lo) * T], I32, (hi - lo) * XB)
             nc.sync.dma_start(
-                out=w2[e][:].bitcast(I32).rearrange("p (g w) -> p g w", g=HP),
-                in_=w2_words[e].bitcast(I32).rearrange("g p w -> p g w"),
+                out=tile[:].rearrange("p (a t) -> p a t", t=T),
+                in_=x_words[lo:hi].rearrange("a p t r -> p a (t r)").bitcast(I32),
             )
+            for a in range(lo, hi):
+                xw[a] = tile[:, (a - lo) * T:(a - lo + 1) * T]
+
+        def load_w1(e, lo, hi):
+            tile = following("w1_%d_%d" % (e, lo), [P, (hi - lo) * WB], U8, (hi - lo) * WB)
+            nc.sync.dma_start(
+                out=tile[:].bitcast(I32).rearrange("p (a w) -> p a w", a=hi - lo),
+                in_=w1_words[e, lo:hi].bitcast(I32).rearrange("a p w -> p a w"),
+            )
+            for a in range(lo, hi):
+                w1[e, a] = tile[:, (a - lo) * WB:(a - lo + 1) * WB]
 
         nc.sync.dma_start(offsets[:], offs)
-        load_x(0, sb("xw0", [P, T], I32))
+        load_x(0, 1)
+        load_scales(xs, x_scales, KP)
+        load_w1(0, 0, 2)
+        load_scales(w1s[0], w1_scales[0], KP)
+        assert cursor[0] == second
         nc.sync.dma_start(
             out=xs_rest[0:64, 0:T].bitcast(I32), in_=x_scales[1:KP].bitcast(I32).rearrange("a f w -> f a w")
         )
-        load_scales(xs0, x_scales[0:1], 1)
-        load_scales(w1s[0], w1_scales[0], KP)
-        load_w1(0, 0)
-        load_x(1, following("xw1", [P, T], I32, XB))
-        load_w1(0, 1)
-        assert cursor[0] == second
-        rest = sb("rest", [P, E * C], U8)
-        nc.vector.tensor_copy(rest[:], xs_rest[:, 0:T_PAD].indirect(offsets[:]))
-        for q in range(4):
-            nc.sync.dma_start(
-                out=moved[32 * q:32 * q + 4, :].bitcast(I32), in_=rest[16 * q:16 * (q + 1), :].bitcast(I32)
-            )
+        ident_part("blank1", second, second + third, 32, 32, nc.vector)
+        zero = sb("zero", [P, 1], F32)
+        nc.vector.memset(zero[:], 0.0)
+        moved = scale_plane("moved", KP - 1, C)
+        load_x(1, 3)
+        load_x(3, 5)
+        load_w1(0, 2, 5)
+        w2_all = following("w2", [P, E * HP * 2 * N], U8, E * HP * 2 * N)
+        nc.sync.dma_start(
+            out=w2_all[:].bitcast(I32).rearrange("p (g w) -> p g w", g=E * HP),
+            in_=w2_words.bitcast(I32).rearrange("e g p w -> p (e g) w"),
+        )
+        w2 = [w2_all[:, e * HP * 2 * N:(e + 1) * HP * 2 * N] for e in range(E)]
         w2s = following("w2s", [P, E * HP * N], U8, E * HP * N)
-        w1s.append(following("w1s1", [P, KP * H], U8, KP * H))
-        for plane in (w2s, w1s[1]):
-            nc.gpsimd.memset(plane[:].bitcast(I32), 0)
-        for a in range(2, KP):
-            load_x(a, following("xw%d" % a, [P, T], I32, XB))
-            load_w1(0, a)
-        load_w2(0)
+        nc.gpsimd.memset(w2s[:].bitcast(I32), 0)
         load_scales(w2s, w2_scales.rearrange("e g q w -> (e g) q w"), E * HP)
+        ident_part("blank2", cursor[0], second + third, 64, 64, nc.gpsimd)
+        load_w1(1, 0, 5)
         gate_sb = following("gate_sb", [P, E * C], F32, 4 * E * C)
         nc.sync.dma_start(out=gate_sb[:], in_=gate[0:P, :])
-        for a in range(KP):
-            load_w1(1, a)
+        w1s.append(following("w1s1", [P, KP * H], U8, KP * H))
+        nc.gpsimd.memset(w1s[1][:].bitcast(I32), 0)
         load_scales(w1s[1], w1_scales[1], KP)
-        load_w2(1)
-        gw_first = following("gw0_0", [P, C], U32, 4 * C)
         assert cursor[0] == second + third
 
         def lst(first, count):
             return offsets[:, first // 16:(first + count) // 16]
 
         def gather_words(dst, a, first, count):
-            nc.vector.tensor_copy(dst, xw[a][:].bitcast(U32).indirect(lst(first, count)))
+            nc.vector.tensor_copy(dst, xw[a].bitcast(U32).indirect(lst(first, count)))
 
         def hidden(acc_t, e, t):
             name = "%d_%d" % (e, t)
             hb = sb("hb" + name, [P, H], BF16)
-            turned = psum.tile([P, HP, 2, P], F32, name="turned" + name, tag="turned", bufs=2)
+            turned = [psum.tile([P, 2, P], F32, name="turned%s_%d" % (name, h), tag="turned", bufs=2) for h in range(HP)]
             for h in range(HP):
                 nc.scalar.activation(
                     out=hb[:, h * PASS:(h + 1) * PASS].rearrange("s (u m j) -> s u m j", u=2, j=2),
@@ -143,27 +147,29 @@ def tile_moe_pkd_mlp_silu_kernel(
                 )
                 for u in range(2):
                     lo = h * 2 * P + u * P
-                    nc.tensor.transpose(turned[:, h, u, :], hb[:].bitcast(F32)[:, lo:lo + P], ident[:])
-            grouped = sb("grouped" + name, [P, HP * P * 4], BF16)
-            nc.scalar.copy(
-                out=grouped[:].bitcast(F32).rearrange("p (g s u) -> p g s u", g=HP, u=2),
-                in_=turned[:].rearrange("p g u s -> p g s u"),
-            )
-            codes = sb("hc" + name, [P, HP * P], U32)
-            scales = sb("hs" + name, [P, HP * P], U8)
-            nc.vector.quantize_mx(out=codes[:].bitcast(FP8X4), scales=scales[:], in_=grouped[:])
+                    nc.tensor.transpose(turned[h][:, u, :], hb[:].bitcast(F32)[:, lo:lo + P], ident[:])
+            codes, scales = [], []
+            for h in range(HP):
+                grouped = sb("grouped%s_%d" % (name, h), [P, P * 4], BF16)
+                nc.scalar.copy(
+                    out=grouped[:].bitcast(F32).rearrange("p (s u) -> p s u", u=2),
+                    in_=turned[h][:].rearrange("p u s -> p s u"),
+                )
+                codes.append(sb("hc%s_%d" % (name, h), [P, P], U32))
+                scales.append(sb("hs%s_%d" % (name, h), [P, P], U8))
+                nc.vector.quantize_mx(out=codes[h][:].bitcast(FP8X4), scales=scales[h][:], in_=grouped[:])
             return codes, scales
 
-        def layer2(e, t, codes, scales):
-            y = psum.tile([P, NT, P], F32, name="y%d_%d" % (e, t), tag="y", bufs=2)
-            for n in range(NT):
+        def layer2(e, t, codes, scales, first_n):
+            y = psum.tile([P, NT // 2, P], F32, name="y%d_%d_%d" % (e, t, first_n), tag="y", bufs=2)
+            for n in range(first_n, first_n + NT // 2):
                 for g in range(HP):
                     nc.tensor.matmul_mx(
-                        out=y[:, n, :],
+                        out=y[:, n - first_n, :],
                         lhsT=w2[e][:, g * 2 * N + n * 2 * P:g * 2 * N + (n + 1) * 2 * P].bitcast(FP4X4),
                         lhsT_scale=w2s[:, (e * HP + g) * N + n * P:(e * HP + g) * N + (n + 1) * P],
-                        rhs=codes[:, g * P:(g + 1) * P].bitcast(FP8X4),
-                        rhs_scale=scales[:, g * P:(g + 1) * P],
+                        rhs=codes[g][:].bitcast(FP8X4),
+                        rhs_scale=scales[g][:],
                         start=(g == 0),
                         stop=(g == HP - 1),
                     )
@@ -179,28 +185,57 @@ def tile_moe_pkd_mlp_silu_kernel(
             nc.scalar.activation(out=res[n][:], in_=zero[:].to_broadcast([P, T]), func=SILU)
 
 
-        gb = [sb("gb%d" % e, [P, C], U8) for e in range(E)]
-        gw = {}
-        for a in range(KP):
+        gw, gb = {}, {}
+
+        def words_of_first_expert(a):
             if a == HOLD:
                 for t in range(ST):
                     gw[t, a] = sb("gw0_%d_%d" % (a, t), [P, P], U32)[:]
                     gather_words(gw[t, a], a, t * P, P)
             else:
-                both = sb("gw0_%d" % a, [P, C], U32) if a else gw_first
+                both = sb("gw0_%d" % a, [P, C], U32)
                 gather_words(both[:], a, 0, C)
                 for t in range(ST):
                     gw[t, a] = both[:, t * P:(t + 1) * P]
-            if a == 0:
-                for e in range(E):
-                    nc.vector.tensor_copy(gb[e][:], xs0[:].indirect(lst(e * C, C)))
 
-        def token_scales(j, a):
-            if a == 0:
-                return gb[j // ST][:, (j % ST) * P:(j % ST + 1) * P]
-            return moved[:, (a - 1) * E * C + j * P:(a - 1) * E * C + (j + 1) * P]
+        def words_of_second_expert(passes, tag):
+            held = sb("gw1_%d" % passes[0], [P, len(passes) * C], U32, tag=tag)
+            for i, a in enumerate(passes):
+                gather_words(held[:, i * C:(i + 1) * C], a, C, C)
+                for t in range(ST):
+                    gw[ST + t, a] = held[:, i * C + t * P:i * C + (t + 1) * P]
+
+        def bytes_in_place(e, a):
+            both = sb("gb%d_%d" % (e, a), [P, C], U8)
+            nc.vector.tensor_copy(both[:], xs[:, a * T:(a + 1) * T].indirect(lst(e * C, C)))
+            for t in range(ST):
+                gb[e * ST + t, a] = both[:, t * P:(t + 1) * P]
+
+        for a in range(KP):
+            words_of_first_expert(a)
+            bytes_in_place(0, a)
+        bytes_in_place(1, 0)
+        rest = sb("rest", [P, C], U8)
+        nc.vector.tensor_copy(rest[:], xs_rest[:, 0:T].indirect(lst(C, C)))
+        for q in range(4):
+            nc.sync.dma_start(
+                out=moved[32 * q:32 * q + 4, :].bitcast(I32), in_=rest[16 * q:16 * (q + 1), :].bitcast(I32)
+            )
+        for a in range(1, KP):
+            for t in range(ST):
+                gb[ST + t, a] = moved[:, (a - 1) * C + t * P:(a - 1) * C + (t + 1) * P]
 
         half = NT // 2
+
+        def finish(j, first_n, y, tag):
+            ysb = sb("ysb%d_%d" % (j, first_n), [P, half, P], F32, tag=tag)
+            nc.scalar.copy(out=ysb[:], in_=y[:])
+            for n in range(first_n, first_n + half):
+                scatter(j, n, ysb[:, n - first_n, :])
+                if j == E * ST - 1:
+                    nc.sync.dma_start(out=out[n * P:(n + 1) * P, :], in_=res[n][:])
+            return ysb
+
         before = None
         for j in range(E * ST):
             e, t = divmod(j, ST)
@@ -210,32 +245,21 @@ def tile_moe_pkd_mlp_silu_kernel(
                     nc.tensor.matmul_mx(
                         out=acc[h][:],
                         lhsT=gw[j, a].bitcast(FP8X4),
-                        lhsT_scale=token_scales(j, a),
+                        lhsT_scale=gb[j, a],
                         rhs=w1[e, a][:, h * 2 * PASS:(h + 1) * 2 * PASS].bitcast(FP4X4),
                         rhs_scale=w1s[e][:, a * H + h * PASS:a * H + (h + 1) * PASS],
                         start=(a == 0),
                         stop=(a == KP - 1),
                     )
             if j == 0:
-                held = sb("gw1", [P, KP * C], U32, tag="gw0_%d_0" % HOLD)
-                for a in range(KP):
-                    gather_words(held[:, a * C:(a + 1) * C], a, C, C)
-                    for i in range(ST):
-                        gw[ST + i, a] = held[:, a * C + i * P:a * C + (i + 1) * P]
+                words_of_second_expert(range(0, SPLIT), "gw0_%d_0" % HOLD)
             codes, scales = hidden(acc, e, t)
+            if j == 0:
+                words_of_second_expert(range(SPLIT, KP), "grouped0_0_1")
             if before is not None:
-                late = sb("late%d" % j, [P, half, P], F32, tag="hb%d_%d" % (e, t))
-                nc.scalar.copy(out=late[:], in_=before[:, half:NT, :])
-                for n in range(half, NT):
-                    scatter(j - 1, n, late[:, n - half, :])
-            y = layer2(e, t, codes, scales)
-            last = j == E * ST - 1
-            first_n = NT if last else half
-            early = sb("early%d" % j, [P, first_n, P], F32)
-            nc.scalar.copy(out=early[:], in_=y[:, 0:first_n, :])
+                finish(j - 1, half, before, "hb%d_%d" % (e, t))
+            y = layer2(e, t, codes, scales, 0)
+            before = layer2(e, t, codes, scales, half)
+            finish(j, 0, y, None)
 
-            for n in range(first_n):
-                scatter(j, n, early[:, n, :])
-                if last:
-                    nc.sync.dma_start(out=out[n * P:(n + 1) * P, :], in_=res[n][:])
-            before = y
+        finish(E * ST - 1, half, before, None)

from contextlib import ExitStack

import concourse.mybir as mybir

K, T, E, C, H, N = 2560, 640, 2, 256, 1024, 512
FLOPS = 2 * E * C * (K * H + H * N)

F32, BF16 = mybir.dt.float32, mybir.dt.bfloat16
I32, U32, U16, U8 = mybir.dt.int32, mybir.dt.uint32, mybir.dt.uint16, mybir.dt.uint8
FP8X4, FP4X4 = mybir.dt.float8_e4m3fn_x4, mybir.dt.float4_e2m1fn_x4
SILU = mybir.ActivationFunctionType.Silu
MULT = mybir.AluOpType.mult

P = 128
PASS = 512
KP, HP = K // PASS, H // PASS
NT = N // P
ST = C // P
HOLD = 2
SPLIT = 3


def tile_moe_pkd_mlp_silu_kernel(
    tc, x_words, x_scales, w1_words, w1_scales, w2_words, w2_scales, gate, offs, out
):
    nc = tc.nc
    with ExitStack() as ctx:
        keep = ctx.enter_context(tc.tile_pool(name="keep", bufs=1))
        staged = ctx.enter_context(tc.tile_pool(name="staged", bufs=1))
        psum = ctx.enter_context(tc.psum_pool(name="psum", bufs=1))

        def sb(name, shape, dtype, tag=None):
            return keep.tile(shape, dtype, name=name, tag=tag or name, align_bytes=64)

        def scale_plane(name, passes, width):
            plane = sb(name, [P, passes * width], U8)
            nc.vector.memset(plane[:].bitcast(I32), 0)
            return plane

        def load_scales(plane, rows, passes):
            src = rows.bitcast(I32).rearrange("a (q r) w -> r q a w", r=4)
            dst = plane[:].bitcast(I32).rearrange("p (a w) -> p a w", a=passes)
            for r in range(4):
                nc.sync.dma_start(out=dst[r:P:32], in_=src[r])

        offsets = keep.tile([P, E * C // 16], U16, name="offsets")
        def placed(name, shape, dtype, offset):
            return staged.tile(shape, dtype, name=name, align_bytes=64, offset=offset)

        XB, WB = 4 * T, 2 * H
        second = 2 * WB
        third = 4 * XB + 3 * WB + KP * WB + E * HP * 2 * N + 4 * E * C + KP * H + E * HP * N
        xs = scale_plane("xs", KP, T)
        ident = sb("ident", [P, P], F32)

        def ident_part(name, offset, end, lo, width, engine):
            zeros = placed(name, [P, (end - offset) // 4], F32, offset)
            engine.memset(zeros[:, 0:width], 0.0)
            nc.gpsimd.affine_select(
                out=ident[:, lo:lo + width], in_=zeros[:, 0:width], compare_op=mybir.AluOpType.not_equal, fill=1.0,
                base=-lo, pattern=[[-1, width]], channel_multiplier=1,
            )

        ident_part("blank0", 0, second, 0, 32, nc.vector)
        w1s = [scale_plane("w1s0", KP, H)]
        xs_rest = scale_plane("xs_rest", 1, T)

        cursor = [0]

        def following(name, shape, dtype, size):
            tile = placed(name, shape, dtype, cursor[0])
            cursor[0] = cursor[0] + size
            return tile

        xw, w1 = {}, {}

        def load_x(lo, hi):
            if lo == 0:
                tile = sb("xw0", [P, T], I32)
            else:
                tile = following("xw%d" % lo, [P, (hi - lo) * T], I32, (hi - lo) * XB)
            nc.sync.dma_start(
                out=tile[:].rearrange("p (a t) -> p a t", t=T),
                in_=x_words[lo:hi].rearrange("a p t r -> p a (t r)").bitcast(I32),
            )
            for a in range(lo, hi):
                xw[a] = tile[:, (a - lo) * T:(a - lo + 1) * T]

        def load_w1(e, lo, hi):
            tile = following("w1_%d_%d" % (e, lo), [P, (hi - lo) * WB], U8, (hi - lo) * WB)
            nc.sync.dma_start(
                out=tile[:].bitcast(I32).rearrange("p (a w) -> p a w", a=hi - lo),
                in_=w1_words[e, lo:hi].bitcast(I32).rearrange("a p w -> p a w"),
            )
            for a in range(lo, hi):
                w1[e, a] = tile[:, (a - lo) * WB:(a - lo + 1) * WB]

        nc.sync.dma_start(offsets[:], offs)
        load_x(0, 1)
        load_scales(xs, x_scales, KP)
        load_w1(0, 0, 2)
        load_scales(w1s[0], w1_scales[0], KP)
        assert cursor[0] == second
        nc.sync.dma_start(
            out=xs_rest[0:64, 0:T].bitcast(I32), in_=x_scales[1:KP].bitcast(I32).rearrange("a f w -> f a w")
        )
        ident_part("blank1", second, second + third, 32, 32, nc.vector)
        zero = sb("zero", [P, 1], F32)
        nc.vector.memset(zero[:], 0.0)
        moved = scale_plane("moved", KP - 1, C)
        load_x(1, 3)
        load_x(3, 5)
        load_w1(0, 2, 5)
        w2_all = following("w2", [P, E * HP * 2 * N], U8, E * HP * 2 * N)
        nc.sync.dma_start(
            out=w2_all[:].bitcast(I32).rearrange("p (g w) -> p g w", g=E * HP),
            in_=w2_words.bitcast(I32).rearrange("e g p w -> p (e g) w"),
        )
        w2 = [w2_all[:, e * HP * 2 * N:(e + 1) * HP * 2 * N] for e in range(E)]
        w2s = following("w2s", [P, E * HP * N], U8, E * HP * N)
        nc.gpsimd.memset(w2s[:].bitcast(I32), 0)
        load_scales(w2s, w2_scales.rearrange("e g q w -> (e g) q w"), E * HP)
        ident_part("blank2", cursor[0], second + third, 64, 64, nc.gpsimd)
        load_w1(1, 0, 5)
        gate_sb = following("gate_sb", [P, E * C], F32, 4 * E * C)
        nc.sync.dma_start(out=gate_sb[:], in_=gate[0:P, :])
        w1s.append(following("w1s1", [P, KP * H], U8, KP * H))
        nc.gpsimd.memset(w1s[1][:].bitcast(I32), 0)
        load_scales(w1s[1], w1_scales[1], KP)
        assert cursor[0] == second + third

        def lst(first, count):
            return offsets[:, first // 16:(first + count) // 16]

        def gather_words(dst, a, first, count):
            nc.vector.tensor_copy(dst, xw[a].bitcast(U32).indirect(lst(first, count)))

        def hidden(acc_t, e, t):
            name = "%d_%d" % (e, t)
            hb = sb("hb" + name, [P, H], BF16)
            turned = [psum.tile([P, 2, P], F32, name="turned%s_%d" % (name, h), tag="turned", bufs=2) for h in range(HP)]
            for h in range(HP):
                nc.scalar.activation(
                    out=hb[:, h * PASS:(h + 1) * PASS].rearrange("s (u m j) -> s u m j", u=2, j=2),
                    in_=acc_t[h][:].rearrange("s (m u j) -> s u m j", u=2, j=2),
                    func=SILU,
                )
                for u in range(2):
                    lo = h * 2 * P + u * P
                    nc.tensor.transpose(turned[h][:, u, :], hb[:].bitcast(F32)[:, lo:lo + P], ident[:])
            codes, scales = [], []
            for h in range(HP):
                grouped = sb("grouped%s_%d" % (name, h), [P, P * 4], BF16)
                nc.scalar.copy(
                    out=grouped[:].bitcast(F32).rearrange("p (s u) -> p s u", u=2),
                    in_=turned[h][:].rearrange("p u s -> p s u"),
                )
                codes.append(sb("hc%s_%d" % (name, h), [P, P], U32))
                scales.append(sb("hs%s_%d" % (name, h), [P, P], U8))
                nc.vector.quantize_mx(out=codes[h][:].bitcast(FP8X4), scales=scales[h][:], in_=grouped[:])
            return codes, scales

        def layer2(e, t, codes, scales, first_n):
            y = psum.tile([P, NT // 2, P], F32, name="y%d_%d_%d" % (e, t, first_n), tag="y", bufs=2)
            for n in range(first_n, first_n + NT // 2):
                for g in range(HP):
                    nc.tensor.matmul_mx(
                        out=y[:, n - first_n, :],
                        lhsT=w2[e][:, g * 2 * N + n * 2 * P:g * 2 * N + (n + 1) * 2 * P].bitcast(FP4X4),
                        lhsT_scale=w2s[:, (e * HP + g) * N + n * P:(e * HP + g) * N + (n + 1) * P],
                        rhs=codes[g][:].bitcast(FP8X4),
                        rhs_scale=scales[g][:],
                        start=(g == 0),
                        stop=(g == HP - 1),
                    )
            return y

        def scatter(j, n, src):
            nc.vector.tensor_tensor(
                res[n][:].indirect(offsets[:, j * P // 16:(j + 1) * P // 16]), src, gate_sb[:, j * P:(j + 1) * P], MULT
            )

        res = [sb("res%d" % n, [P, T], F32) for n in range(NT)]
        for n in range(NT):
            nc.scalar.activation(out=res[n][:], in_=zero[:].to_broadcast([P, T]), func=SILU)


        gw, gb = {}, {}

        def words_of_first_expert(a):
            if a == HOLD:
                for t in range(ST):
                    gw[t, a] = sb("gw0_%d_%d" % (a, t), [P, P], U32)[:]
                    gather_words(gw[t, a], a, t * P, P)
            else:
                both = sb("gw0_%d" % a, [P, C], U32)
                gather_words(both[:], a, 0, C)
                for t in range(ST):
                    gw[t, a] = both[:, t * P:(t + 1) * P]

        def words_of_second_expert(passes, tag):
            held = sb("gw1_%d" % passes[0], [P, len(passes) * C], U32, tag=tag)
            for i, a in enumerate(passes):
                gather_words(held[:, i * C:(i + 1) * C], a, C, C)
                for t in range(ST):
                    gw[ST + t, a] = held[:, i * C + t * P:i * C + (t + 1) * P]

        def bytes_in_place(e, a):
            both = sb("gb%d_%d" % (e, a), [P, C], U8)
            nc.vector.tensor_copy(both[:], xs[:, a * T:(a + 1) * T].indirect(lst(e * C, C)))
            for t in range(ST):
                gb[e * ST + t, a] = both[:, t * P:(t + 1) * P]

        for a in range(KP):
            words_of_first_expert(a)
            bytes_in_place(0, a)
        bytes_in_place(1, 0)
        rest = sb("rest", [P, C], U8)
        nc.vector.tensor_copy(rest[:], xs_rest[:, 0:T].indirect(lst(C, C)))
        for q in range(4):
            nc.sync.dma_start(
                out=moved[32 * q:32 * q + 4, :].bitcast(I32), in_=rest[16 * q:16 * (q + 1), :].bitcast(I32)
            )
        for a in range(1, KP):
            for t in range(ST):
                gb[ST + t, a] = moved[:, (a - 1) * C + t * P:(a - 1) * C + (t + 1) * P]

        half = NT // 2

        def finish(j, first_n, y, tag):
            ysb = sb("ysb%d_%d" % (j, first_n), [P, half, P], F32, tag=tag)
            nc.scalar.copy(out=ysb[:], in_=y[:])
            for n in range(first_n, first_n + half):
                scatter(j, n, ysb[:, n - first_n, :])
                if j == E * ST - 1:
                    nc.sync.dma_start(out=out[n * P:(n + 1) * P, :], in_=res[n][:])
            return ysb

        before = None
        for j in range(E * ST):
            e, t = divmod(j, ST)
            acc = [psum.tile([P, PASS], F32, name="acc%d_%d" % (j, h), tag="acc", bufs=4) for h in range(HP)]
            for a in range(KP):
                for h in range(HP):
                    nc.tensor.matmul_mx(
                        out=acc[h][:],
                        lhsT=gw[j, a].bitcast(FP8X4),
                        lhsT_scale=gb[j, a],
                        rhs=w1[e, a][:, h * 2 * PASS:(h + 1) * 2 * PASS].bitcast(FP4X4),
                        rhs_scale=w1s[e][:, a * H + h * PASS:a * H + (h + 1) * PASS],
                        start=(a == 0),
                        stop=(a == KP - 1),
                    )
            if j == 0:
                words_of_second_expert(range(0, SPLIT), "gw0_%d_0" % HOLD)
            codes, scales = hidden(acc, e, t)
            if j == 0:
                words_of_second_expert(range(SPLIT, KP), "grouped0_0_1")
            if before is not None:
                finish(j - 1, half, before, "hb%d_%d" % (e, t))
            y = layer2(e, t, codes, scales, 0)
            before = layer2(e, t, codes, scales, half)
            finish(j, 0, y, None)

        finish(E * ST - 1, half, before, None)
